import numpy as np
import ml_dtypes


def mxq(x, axis, fmt="e4m3"):
    dtype, down = {"e4m3": (ml_dtypes.float8_e4m3fn, 7), "e5m2": (ml_dtypes.float8_e5m2, 14)}[fmt]
    v = np.moveaxis(np.asarray(x, np.float32).astype(ml_dtypes.bfloat16).astype(np.float64), axis, -1)
    blocks = v.reshape(v.shape[:-1] + (-1, 32))
    amax = np.abs(blocks).max(-1, keepdims=True)
    byte = np.maximum(np.where(amax > 0, np.frexp(amax)[1] - 1 + 127, 0) - down, 1)
    scale = np.exp2(byte - 127.0)
    codes = (blocks / scale).astype(np.float32).astype(dtype).astype(np.float64)
    return np.moveaxis((codes * scale).reshape(v.shape), -1, axis)


WIDE = False


def mx_kscale(k):
    if not WIDE:
        return np.ones(k)
    levels = np.array([10, -10, 5, -5, 0])
    if k % 512:
        return np.exp2(np.random.permutation(np.resize(levels, k // 32))).repeat(32)
    a = np.empty((k // 512, 16))
    for p in range(k // 512):
        a[p, :8] = np.random.permutation(np.resize(levels, 8))
        for g in range(8):
            far = levels[np.abs(levels - a[p, g]) >= 10]
            a[p, g + 8] = far[np.random.randint(len(far))]
    return np.exp2(a.ravel()).repeat(32)


def f64(x):
    return np.asarray(x).astype(np.float64)


def striped(idx):
    return np.tile(idx.reshape(-1, 16).T, (8, 1)).astype(np.uint16)


def unstriped(offs):
    return offs[:16].T.reshape(-1).astype(np.int64)


def striped8(idx):
    return np.concatenate([x.reshape(-1, 16).T for x in idx]).astype(np.uint16)


def runs(offs, k):
    lists = np.stack([offs[16 * r : 16 * r + 16].T.reshape(-1) for r in range(8)]).astype(np.int64)
    return lists[np.arange(k) % 512 // 64]


def pack_weight(w):
    k, n = w.shape
    w = f64(np.asarray(w, np.float32).astype(ml_dtypes.bfloat16)).reshape(k // 32, 32, n)
    amax = np.abs(w).max(1)
    byte = np.clip(np.where(amax > 0, np.frexp(amax)[1] - 1 + 127 - 7, 1), 1, 254)
    scaled = (w * np.exp2(127.0 - byte)[:, None, :]).reshape(k, n).astype(np.float32)
    words = np.ascontiguousarray(scaled.reshape(k // 512, 128, 4, n).transpose(0, 1, 3, 2)).astype(ml_dtypes.float8_e4m3fn).view(np.uint8)
    return words, np.ascontiguousarray(byte.astype(np.uint8).reshape(k // 512, 16, n))


def unpack_weight(words, scales):
    g, p, n, _ = words.shape
    vals = np.ascontiguousarray(words).view(ml_dtypes.float8_e4m3fn).astype(np.float64) * np.repeat(np.exp2(scales.astype(np.float64) - 127.0), 8, axis=1)[..., None]
    return vals.transpose(0, 1, 3, 2).reshape(g * 512, n)


E2M1 = np.array([0.0, 0.5, 1.0, 1.5, 2.0, 3.0, 4.0, 6.0, -0.0, -0.5, -1.0, -1.5, -2.0, -3.0, -4.0, -6.0])


def pack_fp4(w):
    k, n = w.shape
    w = f64(np.asarray(w, np.float32).astype(ml_dtypes.bfloat16)).reshape(k // 32, 32, n)
    amax = np.abs(w).max(1)
    mant, ex = np.frexp(amax / 6.0)
    byte = np.clip(np.where(amax > 0, np.where(mant > 0.5, ex, ex - 1) + 127, 1), 1, 254)
    scaled = (w * np.exp2(127.0 - byte)[:, None, :]).reshape(k, n).astype(np.float32)
    c = np.ascontiguousarray(scaled.reshape(k // 512, 128, 4, n).transpose(0, 1, 3, 2)).astype(ml_dtypes.float4_e2m1fn).view(np.uint8) & 0xF
    words = (c[..., 0::2] | (c[..., 1::2] << 4)).reshape(k // 512, 128, 2 * n)
    return np.ascontiguousarray(words), np.ascontiguousarray(byte.astype(np.uint8).reshape(k // 512, 16, n))


def unpack_fp4(words, scales):
    g, _, n = scales.shape
    words = np.ascontiguousarray(words).reshape(g, 128, n, 2)
    nib = np.empty((g, 128, n, 4), np.uint8)
    nib[..., 0::2] = words & 0xF
    nib[..., 1::2] = words >> 4
    vals = E2M1[nib] * np.repeat(np.exp2(scales.astype(np.float64) - 127.0), 8, axis=1)[..., None]
    return vals.transpose(0, 1, 3, 2).reshape(g * 512, n)


K, T, S, N, G, H, W = 512, 2048, 256, 512, 2048, 512, 128


def setup_inputs():
    n = np.random.standard_normal
    s = mx_kscale(K)[:, None]
    u = mx_kscale(K)
    packed_xT = pack_weight(n((K, T)) * s)
    packed_dT = pack_weight(n((K, G)) / s)
    packed_w1 = pack_fp4(n((H, N)) / np.sqrt(H) / u[:, None])
    perm = np.random.permutation(S)
    perm2 = np.random.permutation(S)
    return {
        "x_words": packed_xT[0],
        "x_scales": packed_xT[1],
        "d_words": packed_dT[0],
        "d_scales": packed_dT[1],
        "gn": (np.random.uniform(0.5, 1.5, (H, 1)) * u[:, None]).astype(np.float32),
        "w1_words": packed_w1[0],
        "w1_scales": packed_w1[1],
        "offs": striped8(np.random.randint(0, T, (8, S))),
        "k1": striped8(np.random.randint(0, G, (8, H))),
        "n1": striped(perm[:W]),
        "n2": striped(perm[W:]),
        "n3": striped(np.random.permutation(S)),
        "n4": striped(perm2[:W]),
        "n5": striped(perm2[W:]),
    }


def reference(x_words, x_scales, d_words, d_scales, gn, w1_words, w1_scales, offs, k1, n1, n2, n3, n4, n5):
    d_k1 = unpack_weight(d_words, d_scales)[np.arange(K)[:, None], runs(k1, K)]
    xq = unpack_weight(x_words, x_scales)[np.arange(K)[:, None], runs(offs, K)]
    h = 0.0625 * (d_k1.T @ xq)
    pa = h[:, unstriped(n1)]
    pb = h[:, unstriped(n2)]
    rb = np.minimum(pa, pb)
    ra = np.maximum(pa, pb)
    ds = np.zeros((H, S))
    ds[:, unstriped(n1)] = ra
    dt = ds.copy()
    dt[:, unstriped(n2)] = rb
    z = f64(gn) * (dt - dt[:, unstriped(n3)])
    h2 = unpack_fp4(w1_words, w1_scales).T @ mxq(z, 0, "e4m3")
    pa2 = h2[:, unstriped(n4)]
    pb2 = h2[:, unstriped(n5)]
    rb2 = pa2 - pb2
    ra2 = 0.75 * (pa2 + pb2)
    ds2 = np.zeros((N, S))
    ds2[:, unstriped(n4)] = ra2
    out = ds2.copy()
    out[:, unstriped(n5)] = rb2
    return out

from contextlib import ExitStack

import concourse.mybir as mybir

K, T, S, N, H, W = 512, 2048, 256, 512, 512, 128
FLOPS = 2 * K * H * S + 2 * H * N * S

F32 = mybir.dt.float32
BF16 = mybir.dt.bfloat16
I32 = mybir.dt.int32
U32 = mybir.dt.uint32
U16 = mybir.dt.uint16
U8 = mybir.dt.uint8
FP8X4 = mybir.dt.float8_e4m3fn_x4
FP4X4 = mybir.dt.float4_e2m1fn_x4
ALU = mybir.AluOpType
COPY = mybir.ActivationFunctionType.Copy

P = 128
PACK = 4
HALF = S // 2


def tile_picked_hpqorddhaar_none_p_kernel(
    tc, x_words, x_scales, d_words, d_scales, gn, w1_words, w1_scales, offs, k1, n1, n2, n3, n4, n5, out
):
    nc = tc.nc
    with ExitStack() as ctx:
        lists = ctx.enter_context(tc.tile_pool(name="lists", bufs=1))
        keep = ctx.enter_context(tc.tile_pool(name="keep", bufs=1))
        psum = ctx.enter_context(tc.psum_pool(name="psum", bufs=1))

        def load_list(src, name):
            tile = lists.tile(list(src.shape), U16, name=name)
            nc.sync.dma_start(tile[:], src)
            return tile

        d_byte_table = keep.tile([P, T], U8, name="d_byte_table")
        x_byte_table = keep.tile([P, T], U8, name="x_byte_table")
        nc.vector.memset(d_byte_table[:].bitcast(I32), 0)
        nc.vector.memset(x_byte_table[:].bitcast(I32), 0)
        placed = keep.tile([P, H + S], U8, name="placed", align_bytes=64)
        nc.vector.memset(placed[:].bitcast(I32), 0)

        k1_t = load_list(k1, "k1")
        offs_t = load_list(offs, "offs")
        n1_t = load_list(n1, "n1")
        n2_t = load_list(n2, "n2")
        d_table = keep.tile([P, T], I32, name="d_table", tag="late2")
        x_table = keep.tile([P, T], I32, name="x_table")
        nc.sync.dma_start(d_byte_table[0:P:8, :].bitcast(I32), d_scales[0].bitcast(I32))
        nc.sync.dma_start(x_byte_table[0:P:8, :].bitcast(I32), x_scales[0].bitcast(I32))
        nc.sync.dma_start(d_table[:], d_words[0].rearrange("p n t -> p (n t)").bitcast(I32))
        nc.sync.dma_start(x_table[:], x_words[0].rearrange("p n t -> p (n t)").bitcast(I32))
        n3_t = load_list(n3, "n3")
        n4_t = load_list(n4, "n4")
        n5_t = load_list(n5, "n5")

        picked_bytes = keep.tile([P, H + S], U8, name="picked_bytes", tag="late0", align_bytes=64)
        nc.vector.tensor_copy(picked_bytes[:, 0:H], d_byte_table[:].indirect(k1_t[:]))
        nc.vector.tensor_copy(picked_bytes[:, H : H + S], x_byte_table[:].indirect(offs_t[:]))
        for s in range(4):
            nc.scalar.dma_start(placed[s:P:32, :].bitcast(I32), picked_bytes[8 * s : P : 32, :].bitcast(I32))

        d_picked = keep.tile([P, H], U32, name="d_picked", tag="late1", align_bytes=64)
        nc.vector.tensor_copy(d_picked[:], d_table[:].bitcast(U32).indirect(k1_t[:]))
        d_codes = keep.tile([P, H], I32, name="d_codes", align_bytes=64)
        nc.vector.tensor_copy(
            d_codes[:].rearrange("p (t b i) -> p b t i", t=PACK, i=4),
            d_picked[:].bitcast(I32).rearrange("p (b i t) -> p b t i", t=PACK, i=4),
        )
        x_codes = keep.tile([P, S], U32, name="x_codes", align_bytes=64)
        nc.vector.tensor_copy(x_codes[:], x_table[:].bitcast(U32).indirect(offs_t[:]))
        d_planes = []
        for t in range(PACK):
            plane = keep.tile([P, P], U8, name=f"d_plane{t}", align_bytes=64)
            nc.vector.tensor_copy(plane[:], placed[:, t:H:PACK])
            d_planes.append(plane[:])

        gain = keep.tile([P, PACK], F32, name="gain", tag="late2")
        nc.sync.dma_start(gain[:], gn.rearrange("(p t) o -> p (t o)", t=PACK))
        w1_codes = keep.tile([P, 2 * N], U8, name="w1_codes", tag="late0", align_bytes=64)
        nc.sync.dma_start(w1_codes[:].bitcast(I32), w1_words[0].bitcast(I32))
        w1_plane = keep.tile([P, N], U8, name="w1_plane", tag="late1", align_bytes=64)
        nc.vector.memset(w1_plane[:].bitcast(I32), 0)
        for q in range(4):
            nc.sync.dma_start(w1_plane[32 * q : 32 * q + 4, :].bitcast(I32), w1_scales[0][4 * q : 4 * q + 4, :].bitcast(I32))

        banks = [psum.tile([P, 512], F32, name=f"bank{b}") for b in range(8)]
        pairs = []
        for t in range(PACK):
            nc.tensor.matmul_mx(
                out=banks[t][:, 0:S],
                lhsT=d_codes[:, t * P : (t + 1) * P].bitcast(FP8X4),
                lhsT_scale=d_planes[t],
                rhs=x_codes[:].bitcast(FP8X4),
                rhs_scale=placed[:, H : H + S],
                start=True,
                stop=True,
            )
            h = keep.tile([P, S], F32, name=f"h{t}")
            if t == 0:
                nc.scalar.activation(h[:], banks[t][:, 0:S], COPY, scale=0.0625)
            else:
                nc.vector.tensor_scalar(h[:], banks[t][:, 0:S], 0.0625, None, ALU.mult)
            pa = keep.tile([P, W], F32, name=f"pa{t}")
            pb = keep.tile([P, W], F32, name=f"pb{t}")
            nc.scalar.activation(pa[:], h[:].indirect(n1_t[:]), COPY)
            nc.scalar.activation(pb[:], h[:].indirect(n2_t[:]), COPY)
            pairs.append((pa, pb))

        gained = []
        for t in range(PACK):
            pa, pb = pairs[t]
            r = keep.tile([P, 2 * W], F32, name=f"r{t}")
            nc.vector.tensor_tensor(r[:, 0:W], pa[:], pb[:], ALU.max)
            nc.vector.tensor_tensor(r[:, W : 2 * W], pa[:], pb[:], ALU.min)
            rg = keep.tile([P, 2 * W], F32, name=f"rg{t}")
            nc.vector.tensor_scalar(rg[:], r[:], gain[:, t : t + 1], None, ALU.mult)
            gained.append(rg)

        dt = [keep.tile([P, S], F32, name=f"dt{t}") for t in range(PACK)]

        def put1(t):
            nc.scalar.activation(dt[t][:].indirect(n1_t[:]), gained[t][:, 0:W], COPY)

        def put2(t):
            nc.scalar.activation(dt[t][:].indirect(n2_t[:]), gained[t][:, W : 2 * W], COPY)
            nc.vector.tensor_copy(near_all[:, t, :], dt[t][:])

        near_all = keep.tile([P, PACK, S], F32, name="near_all")
        far_all = keep.tile([P, PACK, S], F32, name="far_all")

        def fetch(t, j0, w):
            nc.scalar.activation(far_all[:, t, j0 : j0 + w], dt[t][:].indirect(n3_t[:, j0 // 16 : (j0 + w) // 16]), COPY)

        h2 = [keep.tile([P, S], F32, name=f"h2_{u}") for u in range(4)]
        zb = keep.tile([P, S * PACK], BF16, name="zb", align_bytes=64)
        z_codes = keep.tile([P, S], U32, name="z_codes", align_bytes=64)
        z_plane = keep.tile([P, S], U8, name="z_plane", align_bytes=64)

        def quantise(j0, w):
            cols = slice(j0, j0 + w)
            nc.vector.tensor_tensor(
                zb[:, PACK * j0 : PACK * (j0 + w)].rearrange("p (b i t) -> p b t i", t=PACK, i=4),
                near_all[:, :, cols].rearrange("p t (b i) -> p b t i", i=4),
                far_all[:, :, cols].rearrange("p t (b i) -> p b t i", i=4),
                ALU.subtract,
            )
            nc.vector.quantize_mx(out=z_codes[:, cols].bitcast(FP8X4), scales=z_plane[:, cols], in_=zb[:, PACK * j0 : PACK * (j0 + w)])

        def second(c):
            cols = slice(c * HALF, (c + 1) * HALF)
            for u in range(4):
                bank = banks[4 * (1 - c) + u]
                nc.tensor.matmul_mx(
                    out=bank[:, 0:HALF],
                    lhsT=w1_codes[:, 2 * P * u : 2 * P * (u + 1)].bitcast(FP4X4),
                    lhsT_scale=w1_plane[:, P * u : P * (u + 1)],
                    rhs=z_codes[:, cols].bitcast(FP8X4),
                    rhs_scale=z_plane[:, cols],
                    start=True,
                    stop=True,
                )

        def empty(c, u, on_scalar):
            cols = slice(c * HALF, (c + 1) * HALF)
            bank = banks[4 * (1 - c) + u]
            if on_scalar:
                nc.scalar.copy(h2[u][:, cols], bank[:, 0:HALF])
            else:
                nc.vector.tensor_copy(h2[u][:, cols], bank[:, 0:HALF])

        put1(0)
        put1(1)
        put2(0)
        put2(1)
        put1(2)
        put1(3)
        put2(2)
        fetch(0, 0, 128)
        fetch(1, 0, 128)
        put2(3)
        fetch(2, 0, 128)
        fetch(3, 0, 128)
        quantise(0, 128)
        second(0)
        for t in range(3):
            fetch(t, 128, 128)
        fetch(3, 128, 64)
        fetch(3, 192, 64)
        for u in range(4):
            empty(0, u, True)
        quantise(128, 64)
        quantise(192, 64)
        second(1)
        for u in range(4):
            empty(1, u, u == 0)

        mixed = []
        for u in range(4):
            pa2 = keep.tile([P, W], F32, name=f"pa2_{u}")
            pb2 = keep.tile([P, W], F32, name=f"pb2_{u}")
            nc.scalar.activation(pa2[:], h2[u][:].indirect(n4_t[:]), COPY)
            nc.scalar.activation(pb2[:], h2[u][:].indirect(n5_t[:]), COPY)
            r2 = keep.tile([P, 2 * W], F32, name=f"r2_{u}")
            nc.vector.tensor_tensor(r2[:, 0:W], pa2[:], pb2[:], ALU.add)
            nc.vector.tensor_tensor(r2[:, W : 2 * W], pa2[:], pb2[:], ALU.subtract)
            mixed.append(r2)

        res = [keep.tile([P, S], F32, name=f"res{u}") for u in range(4)]
        for u0 in (0, 2):
            for u in (u0, u0 + 1):
                nc.scalar.activation(res[u][:].indirect(n4_t[:]), mixed[u][:, 0:W], COPY, scale=0.75)
            for u in (u0, u0 + 1):
                nc.scalar.activation(res[u][:].indirect(n5_t[:]), mixed[u][:, W : 2 * W], COPY)
                nc.sync.dma_start(out[P * u : P * (u + 1), :], res[u][:])
